import numpy as np
import ml_dtypes


def mxq(x, axis, fmt="e4m3"):
    dtype, down = {"e4m3": (ml_dtypes.float8_e4m3fn, 7), "e5m2": (ml_dtypes.float8_e5m2, 14)}[fmt]
    v = np.moveaxis(np.asarray(x, np.float32).astype(ml_dtypes.bfloat16).astype(np.float64), axis, -1)
    blocks = v.reshape(v.shape[:-1] + (-1, 32))
    amax = np.abs(blocks).max(-1, keepdims=True)
    byte = np.maximum(np.where(amax > 0, np.frexp(amax)[1] - 1 + 127, 0) - down, 1)
    scale = np.exp2(byte - 127.0)
    codes = (blocks / scale).astype(np.float32).astype(dtype).astype(np.float64)
    return np.moveaxis((codes * scale).reshape(v.shape), -1, axis)


WIDE = False


def mx_kscale(k):
    if not WIDE:
        return np.ones(k)
    levels = np.array([10, -10, 5, -5, 0])
    if k % 512:
        return np.exp2(np.random.permutation(np.resize(levels, k // 32))).repeat(32)
    a = np.empty((k // 512, 16))
    for p in range(k // 512):
        a[p, :8] = np.random.permutation(np.resize(levels, 8))
        for g in range(8):
            far = levels[np.abs(levels - a[p, g]) >= 10]
            a[p, g + 8] = far[np.random.randint(len(far))]
    return np.exp2(a.ravel()).repeat(32)


def f64(x):
    return np.asarray(x).astype(np.float64)


def striped(idx):
    return np.tile(idx.reshape(-1, 16).T, (8, 1)).astype(np.uint16)


def unstriped(offs):
    return offs[:16].T.reshape(-1).astype(np.int64)


def striped8(idx):
    return np.concatenate([x.reshape(-1, 16).T for x in idx]).astype(np.uint16)


def runs(offs, k):
    lists = np.stack([offs[16 * r : 16 * r + 16].T.reshape(-1) for r in range(8)]).astype(np.int64)
    return lists[np.arange(k) % 512 // 64]


def pack_weight(w):
    k, n = w.shape
    w = f64(np.asarray(w, np.float32).astype(ml_dtypes.bfloat16)).reshape(k // 32, 32, n)
    amax = np.abs(w).max(1)
    byte = np.clip(np.where(amax > 0, np.frexp(amax)[1] - 1 + 127 - 7, 1), 1, 254)
    scaled = (w * np.exp2(127.0 - byte)[:, None, :]).reshape(k, n).astype(np.float32)
    words = np.ascontiguousarray(scaled.reshape(k // 512, 128, 4, n).transpose(0, 1, 3, 2)).astype(ml_dtypes.float8_e4m3fn).view(np.uint8)
    return words, np.ascontiguousarray(byte.astype(np.uint8).reshape(k // 512, 16, n))


def unpack_weight(words, scales):
    g, p, n, _ = words.shape
    vals = np.ascontiguousarray(words).view(ml_dtypes.float8_e4m3fn).astype(np.float64) * np.repeat(np.exp2(scales.astype(np.float64) - 127.0), 8, axis=1)[..., None]
    return vals.transpose(0, 1, 3, 2).reshape(g * 512, n)


E2M1 = np.array([0.0, 0.5, 1.0, 1.5, 2.0, 3.0, 4.0, 6.0, -0.0, -0.5, -1.0, -1.5, -2.0, -3.0, -4.0, -6.0])


def pack_fp4(w):
    k, n = w.shape
    w = f64(np.asarray(w, np.float32).astype(ml_dtypes.bfloat16)).reshape(k // 32, 32, n)
    amax = np.abs(w).max(1)
    mant, ex = np.frexp(amax / 6.0)
    byte = np.clip(np.where(amax > 0, np.where(mant > 0.5, ex, ex - 1) + 127, 1), 1, 254)
    scaled = (w * np.exp2(127.0 - byte)[:, None, :]).reshape(k, n).astype(np.float32)
    c = np.ascontiguousarray(scaled.reshape(k // 512, 128, 4, n).transpose(0, 1, 3, 2)).astype(ml_dtypes.float4_e2m1fn).view(np.uint8) & 0xF
    words = (c[..., 0::2] | (c[..., 1::2] << 4)).reshape(k // 512, 128, 2 * n)
    return np.ascontiguousarray(words), np.ascontiguousarray(byte.astype(np.uint8).reshape(k // 512, 16, n))


def unpack_fp4(words, scales):
    g, _, n = scales.shape
    words = np.ascontiguousarray(words).reshape(g, 128, n, 2)
    nib = np.empty((g, 128, n, 4), np.uint8)
    nib[..., 0::2] = words & 0xF
    nib[..., 1::2] = words >> 4
    vals = E2M1[nib] * np.repeat(np.exp2(scales.astype(np.float64) - 127.0), 8, axis=1)[..., None]
    return vals.transpose(0, 1, 3, 2).reshape(g * 512, n)


def sigmoid(v):
    return 1.0 / (1.0 + np.exp(-np.maximum(v, -700.0)))

def planes(y):
    n, m = y.shape
    v = y.astype(np.float32).astype(ml_dtypes.bfloat16).astype(np.float64).reshape(n // 32, 32, m)
    top = np.abs(v).max(1)
    byte = np.clip(np.where(top > 0, np.frexp(top)[1] - 1 + 127 - 7, 1), 1, 254)
    codes = (v * np.exp2(127.0 - byte)[:, None, :]).reshape(n, m).astype(np.float32).astype(ml_dtypes.float8_e4m3fn).view(np.uint8)
    words = codes.reshape(n // 512, 128, 4, m).transpose(0, 1, 3, 2)
    return np.ascontiguousarray(words), np.ascontiguousarray(byte.astype(np.uint8).reshape(n // 512, 16, m))


K, T, S, N, G, H, W = 512, 1024, 512, 512, 2048, 512, 256


def setup_inputs():
    n = np.random.standard_normal
    s = mx_kscale(K)[:, None]
    u = mx_kscale(S)
    packed_xT = pack_weight(n((K, T)) * s)
    packed_dT = pack_weight(n((K, G)) / s)
    packed_w1 = pack_fp4(n((H, N)) / np.sqrt(2 * H) / u[:, None])
    packed_w2 = pack_fp4(n((H, N)) / np.sqrt(2 * H) / u[:, None])
    perm = np.random.permutation(S)
    return {
        "x_words": packed_xT[0],
        "x_scales": packed_xT[1],
        "d_words": packed_dT[0],
        "d_scales": packed_dT[1],
        "sl": np.random.uniform(1.0, 2.0, (H, 1)).astype(np.float32),
        "th": (0.5 * n((H, 1))).astype(np.float32),
        "gn": (np.random.uniform(0.5, 1.5, (H, 1)) * u[:, None]).astype(np.float32),
        "gm": (np.random.uniform(0.5, 1.5, (H, 1)) * u[:, None]).astype(np.float32),
        "w1_words": packed_w1[0],
        "w1_scales": packed_w1[1],
        "w2_words": packed_w2[0],
        "w2_scales": packed_w2[1],
        "offs": striped(np.random.permutation(T)[:S]),
        "k1": striped8(np.random.randint(0, G, (8, H))),
        "two": striped(np.random.permutation(T)[:S]),
        "n1": striped(np.random.permutation(S)),
        "n2": striped(np.random.permutation(S)),
        "n3": striped(perm[:W]),
        "n4": striped(perm[W:]),
        "n5": striped(np.random.permutation(S)),
    }


def reference(x_words, x_scales, d_words, d_scales, sl, th, gn, gm, w1_words, w1_scales, w2_words, w2_scales, offs, k1, two, n1, n2, n3, n4, n5):
    d_k1 = unpack_weight(d_words, d_scales)[np.arange(K)[:, None], runs(k1, K)]
    xq = unpack_weight(x_words, x_scales)[:, unstriped(offs)]
    a = 0.0625 * (d_k1.T @ xq)
    st = a - a[:, unstriped(n1)]
    sg = sigmoid(f64(sl) * (st[:, unstriped(n2)] - f64(th)))
    z = f64(gn) * (a * sg)
    x_two = unpack_weight(x_words, x_scales)[:, unstriped(two)]
    b = 0.0625 * (d_k1.T @ x_two)
    pb = b[:, unstriped(n4)]
    pa = b[:, unstriped(n3)]
    rb = pb * sigmoid(pb - pa)
    ra = pa * sigmoid(pa - pb)
    ds = np.zeros((H, S))
    ds[:, unstriped(n3)] = ra
    dt = ds.copy()
    dt[:, unstriped(n4)] = rb
    z2 = f64(gm) * dt
    h = unpack_fp4(w1_words, w1_scales).T @ mxq(z, 0, "e4m3") + unpack_fp4(w2_words, w2_scales).T @ mxq(z2, 0, "e4m3")
    out_0 = h / (np.abs(h[:, unstriped(n5)]) + 0.5)
    return (out_0,) + planes(out_0)

@@ -1,0 +1,430 @@
+from contextlib import ExitStack
+
+import concourse.mybir as mybir
+
+F32 = mybir.dt.float32
+BF16 = mybir.dt.bfloat16
+I32 = mybir.dt.int32
+U32 = mybir.dt.uint32
+U16 = mybir.dt.uint16
+U8 = mybir.dt.uint8
+FP8X4 = mybir.dt.float8_e4m3fn_x4
+FP4X4 = mybir.dt.float4_e2m1fn_x4
+ALU = mybir.AluOpType
+ACT = mybir.ActivationFunctionType
+
+P = 128
+PACK = 4
+S = 512
+HALF = 256
+T = 1024
+G = 2048
+FLOPS = 4 * 2 * 512 * 512 * 512
+
+
+def tile_picked_kjehqduelnorm_none_po_kernel(
+    tc, x_words, x_scales, d_words, d_scales, sl, th, gn, gm, w1_words, w1_scales, w2_words, w2_scales,
+    offs, k1, two, n1, n2, n3, n4, n5, out_0, out_1, out_2,
+):
+    nc = tc.nc
+    with ExitStack() as ctx:
+        sb = ctx.enter_context(tc.tile_pool(name="sb", bufs=1))
+        ps = ctx.enter_context(tc.psum_pool(name="ps", bufs=1))
+
+        def new(name, shape, dtype, tag=None):
+            return sb.tile(shape, dtype, name=name, tag=tag or name, align_bytes=64)
+
+        def load_list(name, src):
+            lst = new(name, list(src.shape), U16)
+            nc.sync.dma_start(lst[:], src)
+            return lst
+
+        def half_of(lst, h):
+            return lst[:, 16 * h : 16 * (h + 1)]
+
+        def cols(h):
+            return slice(HALF * h, HALF * (h + 1))
+
+        def load_scale_rows(queue, plane, src):
+            for j in range(PACK):
+                queue.dma_start(plane[j:P:32, :].bitcast(I32), src[0, j:16:PACK, :].bitcast(I32))
+
+        def deal(engine_copy, dst, src):
+            engine_copy(dst.rearrange("p (t m) -> p m t", t=PACK), src.rearrange("p (m t) -> p m t", t=PACK))
+
+        def interleave(dst, src):
+            nc.vector.tensor_copy(
+                dst[:].rearrange("p (c i t) -> p c t i", i=4, t=PACK),
+                src[:].rearrange("p t (c i) -> p c t i", i=4),
+            )
+
+        d_scale_table = new("d_scale_table", [P, G], U8)
+        x_scale_table = new("x_scale_table", [P, T], U8)
+        key_scales = new("key_scales", [P, S], U8)
+        for plane in (x_scale_table, key_scales):
+            nc.vector.memset(plane[:].bitcast(I32), 0)
+
+        k1_t = load_list("k1_t", k1)
+        nc.sync.dma_start(d_scale_table[:].bitcast(I32), d_scales[0].bitcast(I32).unsqueeze(1).to_broadcast([16, 8, G // 4]))
+        two_t = load_list("two_t", two)
+        x_word_table = new("x_word_table", [P, T], U32)
+        nc.sync.dma_start(x_word_table[:].bitcast(I32), x_words[0].rearrange("p n t -> p (n t)").bitcast(I32))
+        d_word_table = new("d_word_table", [P, G], U32)
+        nc.sync.dma_start(d_word_table[:].bitcast(I32), d_words[0].rearrange("p n t -> p (n t)").bitcast(I32))
+        offs_t = load_list("offs_t", offs)
+        n3_t = load_list("n3_t", n3)
+        n4_t = load_list("n4_t", n4)
+        n1_t = load_list("n1_t", n1)
+        n2_t = load_list("n2_t", n2)
+        n5_t = load_list("n5_t", n5)
+        load_scale_rows(nc.scalar, x_scale_table, x_scales)
+        w_raw = []
+        for i, src in enumerate((w1_words, w2_words)):
+            w_raw.append(new("w_raw%d" % i, [P, 2 * S], U8))
+            nc.gpsimd.dma_start(w_raw[i][:].bitcast(I32), src[0].bitcast(I32))
+
+        key_scale_picked = new("key_scale_picked", [P, S], U8)
+        nc.vector.tensor_copy(key_scale_picked[:], d_scale_table[:].indirect(k1_t[:]))
+        key_scale_dealt = new("key_scale_dealt", [P, S], U8)
+        deal(nc.vector.tensor_copy, key_scale_dealt[:], key_scale_picked[:])
+        for j in range(PACK):
+            nc.scalar.dma_start(key_scales[j:P:32, :].bitcast(I32), key_scale_dealt[8 * j : P : 32, :].bitcast(I32))
+
+        def pick(name, table, lst, dtype, tag=None):
+            picked = new(name, [P, S], dtype, tag=tag)
+            nc.vector.tensor_copy(picked[:], table[:].indirect(lst[:]))
+            return picked
+
+        tok_b_words = pick("tok_b_words", x_word_table, two_t, U32)
+
+        key_picked = new("key_picked", [P, S], U32)
+        nc.vector.tensor_copy(key_picked[:], d_word_table[:].indirect(k1_t[:]))
+        key_words = new("key_words", [P, S], U32)
+        deal(nc.vector.tensor_copy, key_words[:], key_picked[:])
+        tok_b = (tok_b_words, pick("tok_b_scales", x_scale_table, two_t, U8))
+
+        w_scale_raw = new("w_scale_raw", [P, 2 * S], U8, tag="d_word_table")
+        nc.gpsimd.memset(w_scale_raw[:].bitcast(I32), 0)
+        load_scale_rows(nc.sync, w_scale_raw[:, 0:S], w1_scales)
+        load_scale_rows(nc.sync, w_scale_raw[:, S : 2 * S], w2_scales)
+
+        def score(tag, tok):
+            banks = []
+            for t in range(PACK):
+                bank = ps.tile([P, S], F32, name="%s%d" % (tag, t), tag="%s%d" % (tag, t))
+                nc.tensor.matmul_mx(
+                    out=bank[:], lhsT=key_words[:, P * t : P * (t + 1)].bitcast(FP8X4),
+                    lhsT_scale=key_scales[:, P * t : P * (t + 1)],
+                    rhs=tok[0][:].bitcast(FP8X4), rhs_scale=tok[1][:], start=True, stop=True,
+                )
+                banks.append(bank)
+            return banks
+
+        b_bank = score("pb", tok_b)
+        tok_a = (pick("tok_a_words", x_word_table, offs_t, U32, tag="key_picked"), pick("tok_a_scales", x_scale_table, offs_t, U8, tag="key_scale_picked"))
+        a_bank = score("pa", tok_a)
+
+        rows = {}
+        for name, src, tag in (("gm", gm, "tok_b_words"), ("sl", sl, "tok_b_scales"), ("th", th, "x_word_table"), ("gn", gn, "x_scale_table")):
+            rows[name] = new(name + "_t", [P, PACK], F32, tag=tag)
+            nc.sync.dma_start(rows[name][:], src.rearrange("(p t) o -> p (t o)", t=PACK))
+        w_words = []
+        for i in range(2):
+            w_words.append(new("w_words%d" % i, [P, 2 * S], U8))
+            deal(nc.scalar.copy, w_words[i][:].bitcast(U16), w_raw[i][:].bitcast(U16))
+
+        sig_bias = new("sig_bias", [P, PACK], F32)
+        gn16 = new("gn16", [P, PACK], F32)
+
+        def row_constants():
+            nc.vector.scalar_tensor_tensor(sig_bias[:], rows["sl"][:], -1.0, rows["th"][:], ALU.mult, ALU.mult)
+            nc.vector.tensor_scalar(gn16[:], rows["gn"][:], 0.0625, None, ALU.mult)
+
+        def gather(on_scalar, dst, window, lst):
+            if on_scalar:
+                nc.scalar.activation(dst, window[:].indirect(lst), ACT.Copy)
+            else:
+                nc.vector.tensor_copy(dst, window[:].indirect(lst))
+
+        def per_tile(name, width, dtype=F32):
+            return [new("%s%d" % (name, t), [P, width], dtype) for t in range(PACK)]
+
+        b_win, a_win, st_win, dt_win, r_win = (per_tile(n, S) for n in ("b_win", "a_win", "st_win", "dt_win", "r_win"))
+        pa, pb, diff, sa, sbm, ra, rb = (per_tile(n, HALF) for n in ("pa_", "pb_", "diff", "sa", "sbm", "ra", "rb"))
+        a_n1 = per_tile("a_n1", S)
+        z2_planes = new("z2_planes", [P, PACK, S], BF16)
+
+        def evac_b(t):
+            nc.scalar.activation(b_win[t][:], b_bank[t][:], ACT.Copy, scale=0.0625)
+
+        def evac_a(t):
+            nc.scalar.activation(a_win[t][:], a_bank[t][:], ACT.Copy, scale=0.0625)
+
+        def evac_a_vector(t):
+            nc.vector.tensor_scalar(a_win[t][:], a_bank[t][:], 0.0625, None, ALU.mult)
+
+        def fetch_pairs(t, on_scalar):
+            gather(on_scalar, pa[t][:], b_win[t], n3_t[:])
+            gather(on_scalar, pb[t][:], b_win[t], n4_t[:])
+
+        def differ(t):
+            nc.vector.tensor_tensor(diff[t][:], pa[t][:], pb[t][:], ALU.subtract)
+
+        def differ_g(t):
+            nc.gpsimd.tensor_tensor(diff[t][:], pa[t][:], pb[t][:], ALU.subtract)
+
+        def product_g(t, side):
+            r_, p_, s_ = ((ra, pa, sa), (rb, pb, sbm))[side]
+            nc.gpsimd.tensor_tensor(r_[t][:], p_[t][:], s_[t][:], ALU.mult)
+
+        def put_copy(t, side):
+            lst, r_ = ((n3_t, ra), (n4_t, rb))[side]
+            nc.vector.tensor_copy(dt_win[t][:].indirect(lst[:]), r_[t][:])
+
+        def regroup_scalar(t):
+            nc.scalar.activation(z2_planes[:, t, :], dt_win[t][:], ACT.Copy, scale=rows["gm"][:, t : t + 1])
+
+        def regroup_g(t):
+            nc.gpsimd.tensor_scalar(z2_planes[:, t, :], dt_win[t][:], rows["gm"][:, t : t + 1], 0.0, ALU.mult, ALU.add)
+
+        def duel(t):
+            nc.scalar.activation(sa[t][:], diff[t][:], ACT.Sigmoid)
+            nc.scalar.activation(sbm[t][:], diff[t][:], ACT.Sigmoid, scale=-1.0)
+
+        def put_vector(t, side):
+            lst, p_, s_ = ((n3_t, pa, sa), (n4_t, pb, sbm))[side]
+            nc.vector.tensor_tensor(dt_win[t][:].indirect(lst[:]), p_[t][:], s_[t][:], ALU.mult)
+
+        def products(t):
+            nc.vector.tensor_tensor(ra[t][:], pa[t][:], sa[t][:], ALU.mult)
+            nc.vector.tensor_tensor(rb[t][:], pb[t][:], sbm[t][:], ALU.mult)
+
+        def put_scalar(t, side):
+            lst, r_ = ((n3_t, ra), (n4_t, rb))[side]
+            nc.scalar.activation(dt_win[t][:].indirect(lst[:]), r_[t][:], ACT.Copy)
+
+        def regroup(t):
+            nc.vector.tensor_scalar(z2_planes[:, t, :], dt_win[t][:], rows["gm"][:, t : t + 1], None, ALU.mult)
+
+        def fetch_n1(t, on_scalar):
+            for h in range(2):
+                gather(on_scalar, a_n1[t][:, cols(h)], a_win[t], half_of(n1_t, h))
+
+        def step(t):
+            nc.vector.scalar_tensor_tensor(st_win[t][:], a_bank[t][:], 0.0625, a_n1[t][:], ALU.mult, ALU.subtract)
+
+        w_scales = new("w_scales", [P, 2 * S], U8)
+
+        def deal_w_scales():
+            nc.vector.tensor_copy(
+                w_scales[:].rearrange("p (w t m) -> p w m t", w=2, t=PACK),
+                w_scale_raw[:].rearrange("p (w m t) -> p w m t", w=2, t=PACK),
+            )
+
+        def w_pass(bank, i, t, codes, scales, start, stop):
+            nc.tensor.matmul_mx(
+                out=bank, lhsT=w_words[i][:, 2 * P * t : 2 * P * (t + 1)].bitcast(FP4X4),
+                lhsT_scale=w_scales[:, S * i + P * t : S * i + P * (t + 1)],
+                rhs=codes.bitcast(FP8X4), rhs_scale=scales, start=start, stop=stop,
+            )
+
+        h_bank = [[], []]
+        z2_packed = new("z2_packed", [P, PACK * S], BF16)
+        z2_codes = new("z2_codes", [P, S], U32)
+        z2_scales = new("z2_scales", [P, S], U8)
+
+        def pack_z2():
+            interleave(z2_packed, z2_planes)
+
+        def pack_z2_g(h):
+            nc.gpsimd.tensor_scalar(
+                z2_packed[:, PACK * HALF * h : PACK * HALF * (h + 1)].rearrange("p (c t) -> p c t", t=PACK),
+                z2_planes[:, :, cols(h)].rearrange("p t c -> p c t"), 1.0, 0.0, ALU.mult, ALU.add,
+            )
+
+        def quant_z2_half(h):
+            nc.vector.quantize_mx(
+                out=z2_codes[:, cols(h)].bitcast(FP8X4), scales=z2_scales[:, cols(h)],
+                in_=z2_packed[:, PACK * HALF * h : PACK * HALF * (h + 1)],
+            )
+
+        def quant_z2():
+            nc.vector.quantize_mx(out=z2_codes[:].bitcast(FP8X4), scales=z2_scales[:], in_=z2_packed[:])
+
+        sg = [new("sg%d" % h, [P, PACK, HALF], F32) for h in range(2)]
+        z_planes = [new("z_planes%d" % h, [P, PACK, HALF], BF16) for h in range(2)]
+        z_packed = [new("z_packed%d" % h, [P, PACK * HALF], BF16) for h in range(2)]
+
+        def gate(h, t):
+            nc.scalar.activation(
+                sg[h][:, t, :], st_win[t][:].indirect(half_of(n2_t, h)), ACT.Sigmoid,
+                bias=sig_bias[:, t : t + 1], scale=rows["sl"][:, t : t + 1],
+            )
+
+        def gated(h, t):
+            nc.vector.scalar_tensor_tensor(
+                z_planes[h][:, t, :], a_bank[t][:, cols(h)], gn16[:, t : t + 1], sg[h][:, t, :], ALU.mult, ALU.mult
+            )
+
+        def pack_z(h):
+            interleave(z_packed[h], z_planes[h])
+
+        def quant_z(h):
+            z_codes = new("z_codes%d" % h, [P, HALF], U32)
+            z_scales = new("z_scales%d" % h, [P, HALF], U8)
+            nc.vector.quantize_mx(out=z_codes[:].bitcast(FP8X4), scales=z_scales[:], in_=z_packed[h][:])
+            for t in range(PACK):
+                h_bank[h].append(ps.tile([P, S], F32, name="ph%d_%d" % (h, t), tag=("pb%d", "pa%d")[h] % t)[:, 0:HALF])
+                w_pass(h_bank[h][t], 1, t, z2_codes[:, cols(h)], z2_scales[:, cols(h)], True, False)
+                w_pass(h_bank[h][t], 0, t, z_codes[:], z_scales[:], False, True)
+
+        size = per_tile("size", S)
+        root = per_tile("root", S)
+
+        def absolute(h, t):
+            nc.scalar.activation(size[t][:, cols(h)], h_bank[h][t], ACT.Abs)
+
+        def inverse_root(t, c):
+            nc.scalar.activation(root[t][:, c], size[t][:, c], ACT.Abs_reciprocal_sqrt, bias=0.5)
+
+        def square(t, c, engine):
+            engine.tensor_tensor(r_win[t][:, c], root[t][:, c], root[t][:, c], ALU.mult)
+
+        out_rows = out_0.rearrange("(p t) j -> p t j", t=PACK)
+        y_codes = new("y_codes", [P, S], U32)
+        y_scales = new("y_scales", [P, S], U8)
+        code_rows = out_1[0].rearrange("p n t -> p (n t)").bitcast(I32)
+        r_n5 = [new("r_n5_%d" % h, [P, PACK, HALF], F32) for h in range(2)]
+        y = [new("y%d" % h, [P, PACK, HALF], F32) for h in range(2)]
+        y_packed = [new("y_packed%d" % h, [P, PACK * HALF], BF16) for h in range(2)]
+
+        def fetch_n5(h, t, on_scalar):
+            gather(on_scalar, r_n5[h][:, t, :], r_win[t], half_of(n5_t, h))
+
+        def result(h, t):
+            nc.vector.tensor_tensor(y[h][:, t, :], h_bank[h][t], r_n5[h][:, t, :], ALU.mult)
+
+        def store_y(h):
+            nc.sync.dma_start(out_rows[:, :, cols(h)], y[h][:])
+
+        def pack_y(h):
+            interleave(y_packed[h], y[h])
+
+        def quant_y(h):
+            nc.vector.quantize_mx(out=y_codes[:, cols(h)].bitcast(FP8X4), scales=y_scales[:, cols(h)], in_=y_packed[h][:])
+            nc.sync.dma_start(code_rows[:, cols(h)], y_codes[:, cols(h)].bitcast(I32))
+
+        evac_b(0)
+        fetch_pairs(0, True)
+        evac_b(1)
+        differ(0)
+        evac_a_vector(0)
+        duel(0)
+        fetch_n1(0, False)
+        put_vector(0, 0)
+        fetch_pairs(1, True)
+        differ_g(1)
+        evac_b(2)
+        step(0)
+        put_vector(0, 1)
+        duel(1)
+        product_g(1, 0)
+        product_g(1, 1)
+        regroup(0)
+        fetch_pairs(2, True)
+        differ_g(2)
+        evac_b(3)
+        put_copy(1, 0)
+        duel(2)
+        product_g(2, 0)
+        product_g(2, 1)
+        fetch_pairs(3, True)
+        differ_g(3)
+        put_copy(1, 1)
+        evac_a(1)
+        regroup(1)
+        duel(3)
+        product_g(3, 0)
+        product_g(3, 1)
+        fetch_n1(1, True)
+        put_copy(2, 0)
+        evac_a(2)
+        step(1)
+        put_scalar(3, 0)
+        put_copy(2, 1)
+        deal_w_scales()
+        row_constants()
+        regroup(2)
+        put_scalar(3, 1)
+        regroup_scalar(3)
+        fetch_n1(2, True)
+        pack_z2_g(0)
+        pack_z2_g(1)
+        step(2)
+        evac_a(3)
+        fetch_n1(3, True)
+        quant_z2_half(0)
+        step(3)
+        gate(0, 0)
+        gate(0, 1)
+        gate(0, 2)
+        quant_z2_half(1)
+        gate(0, 3)
+        gated(0, 0)
+        gated(0, 1)
+        gated(0, 2)
+        gated(0, 3)
+        gate(1, 0)
+        pack_z(0)
+        gate(1, 1)
+        quant_z(0)
+        gated(1, 0)
+        gate(1, 2)
+        gated(1, 1)
+        gate(1, 3)
+        gated(1, 2)
+        gated(1, 3)
+        pack_z(1)
+        quant_z(1)
+        absolute(0, 0)
+        inverse_root(0, cols(0))
+        absolute(1, 0)
+        inverse_root(0, cols(1))
+        square(0, slice(0, S), nc.vector)
+        absolute(0, 1)
+        absolute(1, 1)
+        inverse_root(1, slice(0, S))
+        fetch_n5(0, 0, False)
+        square(1, slice(0, S), nc.vector)
+        absolute(0, 2)
+        absolute(1, 2)
+        inverse_root(2, slice(0, S))
+        result(0, 0)
+        fetch_n5(0, 1, False)
+        square(2, slice(0, S), nc.gpsimd)
+        absolute(0, 3)
+        absolute(1, 3)
+        inverse_root(3, slice(0, S))
+        result(0, 1)
+        square(3, slice(0, S), nc.gpsimd)
+        fetch_n5(1, 0, False)
+        result(1, 0)
+        fetch_n5(0, 2, True)
+        fetch_n5(1, 1, False)
+        fetch_n5(0, 3, True)
+        result(0, 2)
+        result(0, 3)
+        store_y(0)
+        fetch_n5(1, 2, True)
+        pack_y(0)
+        fetch_n5(1, 3, True)
+        result(1, 1)
+        quant_y(0)
+        result(1, 2)
+        result(1, 3)
+        store_y(1)
+        pack_y(1)
+        quant_y(1)
+        for j in range(PACK):
+            queue = nc.scalar if j % 2 else nc.sync
+            queue.dma_start(out_2[0, j:16:PACK, :].bitcast(I32), y_scales[j:P:32, :].bitcast(I32))

@@ -55,7 +55,7 @@ def tile_picked_kjehqduelnorm_none_po_kernel(
         def interleave(dst, src):
             nc.vector.tensor_copy(
                 dst[:].rearrange("p (c i t) -> p c t i", i=4, t=PACK),
-                src[:].rearrange("p t (c i) -> p c t i", i=4),
+                src.rearrange("p t (c i) -> p c t i", i=4),
             )
 
         d_scale_table = new("d_scale_table", [P, G], U8)
@@ -149,7 +149,7 @@ def tile_picked_kjehqduelnorm_none_po_kernel(
         def per_tile(name, width, dtype=F32):
             return [new("%s%d" % (name, t), [P, width], dtype) for t in range(PACK)]
 
-        b_win, a_win, st_win, dt_win, r_win = (per_tile(n, S) for n in ("b_win", "a_win", "st_win", "dt_win", "r_win"))
+        b_win, a_win, st_win, dt_win = (per_tile(n, S) for n in ("b_win", "a_win", "st_win", "dt_win"))
         pa, pb, diff, sa, sbm, ra, rb = (per_tile(n, HALF) for n in ("pa_", "pb_", "diff", "sa", "sbm", "ra", "rb"))
         a_n1 = per_tile("a_n1", S)
         z2_planes = new("z2_planes", [P, PACK, S], BF16)
@@ -229,31 +229,23 @@ def tile_picked_kjehqduelnorm_none_po_kernel(
             )
 
         h_bank = [[], []]
-        z2_packed = new("z2_packed", [P, PACK * S], BF16)
+        z2_packed = [new("z2_packed%d" % h, [P, PACK * HALF], BF16, tag="a_n1%d" % (2 + h)) for h in range(2)]
         z2_codes = new("z2_codes", [P, S], U32)
         z2_scales = new("z2_scales", [P, S], U8)
 
-        def pack_z2():
-            interleave(z2_packed, z2_planes)
+        def pack_z2(h):
+            interleave(z2_packed[h], z2_planes[:, :, cols(h)])
 
-        def pack_z2_g(h):
-            nc.gpsimd.tensor_scalar(
-                z2_packed[:, PACK * HALF * h : PACK * HALF * (h + 1)].rearrange("p (c t) -> p c t", t=PACK),
-                z2_planes[:, :, cols(h)].rearrange("p t c -> p c t"), 1.0, 0.0, ALU.mult, ALU.add,
-            )
-
-        def quant_z2_half(h):
-            nc.vector.quantize_mx(
-                out=z2_codes[:, cols(h)].bitcast(FP8X4), scales=z2_scales[:, cols(h)],
-                in_=z2_packed[:, PACK * HALF * h : PACK * HALF * (h + 1)],
-            )
-
-        def quant_z2():
-            nc.vector.quantize_mx(out=z2_codes[:].bitcast(FP8X4), scales=z2_scales[:], in_=z2_packed[:])
+        def quant_z2(h):
+            nc.vector.quantize_mx(out=z2_codes[:, cols(h)].bitcast(FP8X4), scales=z2_scales[:, cols(h)], in_=z2_packed[h][:])
 
         sg = [new("sg%d" % h, [P, PACK, HALF], F32) for h in range(2)]
         z_planes = [new("z_planes%d" % h, [P, PACK, HALF], BF16) for h in range(2)]
         z_packed = [new("z_packed%d" % h, [P, PACK * HALF], BF16) for h in range(2)]
+
+        z_codes = [new("z_codes%d" % h, [P, HALF], U32) for h in range(2)]
+        z_scales = [new("z_scales%d" % h, [P, HALF], U8) for h in range(2)]
+        r_win = [new("r_win%d" % t, [P, S], F32, tag=tag) for t, tag in enumerate(("z_packed1", "z_codes1", "z_scales1", "z2_codes"))]
 
         def gate(h, t):
             nc.scalar.activation(
@@ -267,25 +259,23 @@ def tile_picked_kjehqduelnorm_none_po_kernel(
             )
 
         def pack_z(h):
-            interleave(z_packed[h], z_planes[h])
+            interleave(z_packed[h], z_planes[h][:])
 
         def quant_z(h):
-            z_codes = new("z_codes%d" % h, [P, HALF], U32)
-            z_scales = new("z_scales%d" % h, [P, HALF], U8)
-            nc.vector.quantize_mx(out=z_codes[:].bitcast(FP8X4), scales=z_scales[:], in_=z_packed[h][:])
+            nc.vector.quantize_mx(out=z_codes[h][:].bitcast(FP8X4), scales=z_scales[h][:], in_=z_packed[h][:])
             for t in range(PACK):
                 h_bank[h].append(ps.tile([P, S], F32, name="ph%d_%d" % (h, t), tag=("pb%d", "pa%d")[h] % t)[:, 0:HALF])
                 w_pass(h_bank[h][t], 1, t, z2_codes[:, cols(h)], z2_scales[:, cols(h)], True, False)
-                w_pass(h_bank[h][t], 0, t, z_codes[:], z_scales[:], False, True)
+                w_pass(h_bank[h][t], 0, t, z_codes[h][:], z_scales[h][:], False, True)
 
-        size = per_tile("size", S)
+        size = [[new("size%d_%d" % (h, t), [P, HALF], F32, tag="size%d_%d" % (h, t % 2)) for t in range(PACK)] for h in range(2)]
         root = per_tile("root", S)
 
         def absolute(h, t):
-            nc.scalar.activation(size[t][:, cols(h)], h_bank[h][t], ACT.Abs)
+            nc.scalar.activation(size[h][t][:], h_bank[h][t], ACT.Abs)
 
-        def inverse_root(t, c):
-            nc.scalar.activation(root[t][:, c], size[t][:, c], ACT.Abs_reciprocal_sqrt, bias=0.5)
+        def inverse_root(h, t):
+            nc.scalar.activation(root[t][:, cols(h)], size[h][t][:], ACT.Abs_reciprocal_sqrt, bias=0.5)
 
         def square(t, c, engine):
             engine.tensor_tensor(r_win[t][:, c], root[t][:, c], root[t][:, c], ALU.mult)
@@ -308,7 +298,7 @@ def tile_picked_kjehqduelnorm_none_po_kernel(
             nc.sync.dma_start(out_rows[:, :, cols(h)], y[h][:])
 
         def pack_y(h):
-            interleave(y_packed[h], y[h])
+            interleave(y_packed[h], y[h][:])
 
         def quant_y(h):
             nc.vector.quantize_mx(out=y_codes[:, cols(h)].bitcast(FP8X4), scales=y_scales[:, cols(h)], in_=y_packed[h][:])
@@ -317,109 +307,111 @@ def tile_picked_kjehqduelnorm_none_po_kernel(
         evac_b(0)
         fetch_pairs(0, True)
         evac_b(1)
-        differ(0)
-        evac_a_vector(0)
-        duel(0)
-        fetch_n1(0, False)
-        put_vector(0, 0)
-        fetch_pairs(1, True)
-        differ_g(1)
         evac_b(2)
-        step(0)
-        put_vector(0, 1)
-        duel(1)
-        product_g(1, 0)
-        product_g(1, 1)
-        regroup(0)
-        fetch_pairs(2, True)
-        differ_g(2)
+        differ(0)
+        fetch_pairs(1, False)
         evac_b(3)
-        put_copy(1, 0)
-        duel(2)
-        product_g(2, 0)
-        product_g(2, 1)
         fetch_pairs(3, True)
-        differ_g(3)
-        put_copy(1, 1)
-        evac_a(1)
-        regroup(1)
+        differ(1)
+        fetch_pairs(2, False)
+        duel(1)
+        differ(3)
+        differ(2)
+        duel(0)
+        put_vector(1, 0)
+        products(0)
+        duel(2)
         duel(3)
-        product_g(3, 0)
-        product_g(3, 1)
+        put_vector(1, 1)
+        evac_a(0)
+        fetch_n1(0, True)
+        put_vector(2, 0)
+        put_scalar(0, 0)
+        evac_a(1)
+        put_vector(2, 1)
+        put_scalar(0, 1)
+        regroup_scalar(0)
+        put_vector(3, 0)
         fetch_n1(1, True)
-        put_copy(2, 0)
+        regroup(1)
+        regroup(2)
+        put_vector(3, 1)
         evac_a(2)
+        fetch_n1(2, True)
+        step(0)
         step(1)
-        put_scalar(3, 0)
-        put_copy(2, 1)
         deal_w_scales()
         row_constants()
-        regroup(2)
-        put_scalar(3, 1)
-        regroup_scalar(3)
-        fetch_n1(2, True)
-        pack_z2_g(0)
-        pack_z2_g(1)
-        step(2)
+        regroup(3)
         evac_a(3)
         fetch_n1(3, True)
-        quant_z2_half(0)
+        step(2)
         step(3)
+        pack_z2(0)
         gate(0, 0)
         gate(0, 1)
         gate(0, 2)
-        quant_z2_half(1)
         gate(0, 3)
         gated(0, 0)
+        quant_z2(0)
         gated(0, 1)
         gated(0, 2)
         gated(0, 3)
         gate(1, 0)
         pack_z(0)
         gate(1, 1)
-        quant_z(0)
         gated(1, 0)
+        quant_z(0)
+        pack_z2(1)
         gate(1, 2)
         gated(1, 1)
+        quant_z2(1)
         gate(1, 3)
         gated(1, 2)
         gated(1, 3)
         pack_z(1)
         quant_z(1)
         absolute(0, 0)
-        inverse_root(0, cols(0))
-        absolute(1, 0)
-        inverse_root(0, cols(1))
-        square(0, slice(0, S), nc.vector)
+        inverse_root(0, 0)
+        square(0, cols(0), nc.vector)
         absolute(0, 1)
-        absolute(1, 1)
-        inverse_root(1, slice(0, S))
-        fetch_n5(0, 0, False)
-        square(1, slice(0, S), nc.vector)
+        inverse_root(0, 1)
+        square(1, cols(0), nc.vector)
         absolute(0, 2)
-        absolute(1, 2)
-        inverse_root(2, slice(0, S))
-        result(0, 0)
-        fetch_n5(0, 1, False)
-        square(2, slice(0, S), nc.gpsimd)
+        inverse_root(0, 2)
+        square(2, cols(0), nc.vector)
         absolute(0, 3)
+        inverse_root(0, 3)
+        square(3, cols(0), nc.vector)
+        absolute(1, 0)
+        inverse_root(1, 0)
+        square(0, cols(1), nc.vector)
+        absolute(1, 1)
+        inverse_root(1, 1)
+        fetch_n5(0, 0, False)
+        square(1, cols(1), nc.vector)
+        absolute(1, 2)
+        inverse_root(1, 2)
+        result(0, 0)
+        square(2, cols(1), nc.vector)
         absolute(1, 3)
-        inverse_root(3, slice(0, S))
-        result(0, 1)
-        square(3, slice(0, S), nc.gpsimd)
-        fetch_n5(1, 0, False)
-        result(1, 0)
+        inverse_root(1, 3)
+        fetch_n5(0, 1, False)
+        square(3, cols(1), nc.vector)
         fetch_n5(0, 2, True)
-        fetch_n5(1, 1, False)
+        result(0, 1)
         fetch_n5(0, 3, True)
         result(0, 2)
+        fetch_n5(1, 0, True)
         result(0, 3)
         store_y(0)
-        fetch_n5(1, 2, True)
         pack_y(0)
-        fetch_n5(1, 3, True)
-        result(1, 1)
+        fetch_n5(1, 1, True)
+        result(1, 0)
         quant_y(0)
+        fetch_n5(1, 2, True)
+        result(1, 1)
+        fetch_n5(1, 3, True)
         result(1, 2)
         result(1, 3)
         store_y(1)

@@ -83,6 +83,10 @@ def tile_picked_kjehqduelnorm_none_po_kernel(
             w_raw.append(new("w_raw%d" % i, [P, 2 * S], U8))
             nc.gpsimd.dma_start(w_raw[i][:].bitcast(I32), src[0].bitcast(I32))
 
+        spare_in = new("spare_in", [P, 1], F32)
+        nc.vector.memset(spare_in[:], 0.0)
+        spare_sig = new("spare_sig", [P, 1], F32)
+        nc.scalar.activation(spare_sig[:], spare_in[:], ACT.Sigmoid)
         key_scale_picked = new("key_scale_picked", [P, S], U8)
         nc.vector.tensor_copy(key_scale_picked[:], d_scale_table[:].indirect(k1_t[:]))
         key_scale_dealt = new("key_scale_dealt", [P, S], U8)
@@ -271,6 +275,10 @@ def tile_picked_kjehqduelnorm_none_po_kernel(
         size = [[new("size%d_%d" % (h, t), [P, HALF], F32, tag="size%d_%d" % (h, t % 2)) for t in range(PACK)] for h in range(2)]
         root = per_tile("root", S)
 
+        def warm_root():
+            spare_root = new("spare_root", [P, 1], F32)
+            nc.scalar.activation(spare_root[:], sg[1][:, PACK - 1, 0:1], ACT.Abs_reciprocal_sqrt, bias=0.5)
+
         def absolute(h, t):
             nc.scalar.activation(size[h][t][:], h_bank[h][t], ACT.Abs)
 
@@ -367,6 +375,7 @@ def tile_picked_kjehqduelnorm_none_po_kernel(
         gated(1, 1)
         quant_z2(1)
         gate(1, 3)
+        warm_root()
         gated(1, 2)
         gated(1, 3)
         pack_z(1)

@@ -16,10 +16,16 @@ ACT = mybir.ActivationFunctionType
 P = 128
 PACK = 4
 S = 512
-HALF = 256
+HALF = S // 2
 T = 1024
 G = 2048
+SCALE_ROWS = 16
+SCORE = 0.0625
 FLOPS = 4 * 2 * 512 * 512 * 512
+
+PAIRS_ON_VECTOR = (1, 2)
+SCATTER_ON_SCALAR = 0
+LATE_TILES = (2, 3)
 
 
 def tile_picked_kjehqduelnorm_none_po_kernel(
@@ -27,12 +33,20 @@ def tile_picked_kjehqduelnorm_none_po_kernel(
     offs, k1, two, n1, n2, n3, n4, n5, out_0, out_1, out_2,
 ):
     nc = tc.nc
+    tiles = range(PACK)
+    halves = range(2)
     with ExitStack() as ctx:
-        sb = ctx.enter_context(tc.tile_pool(name="sb", bufs=1))
-        ps = ctx.enter_context(tc.psum_pool(name="ps", bufs=1))
+        sbuf = ctx.enter_context(tc.tile_pool(name="sbuf", bufs=1))
+        psum = ctx.enter_context(tc.psum_pool(name="psum", bufs=1))
 
-        def new(name, shape, dtype, tag=None):
-            return sb.tile(shape, dtype, name=name, tag=tag or name, align_bytes=64)
+        def new(name, shape, dtype, reuse=None):
+            return sbuf.tile(shape, dtype, name=name, tag=reuse or name, align_bytes=64)
+
+        def per_tile(name, width):
+            return [new("%s%d" % (name, t), [P, width], F32) for t in tiles]
+
+        def cols(h):
+            return slice(HALF * h, HALF * (h + 1))
 
         def load_list(name, src):
             lst = new(name, list(src.shape), U16)
@@ -40,23 +54,32 @@ def tile_picked_kjehqduelnorm_none_po_kernel(
             return lst
 
         def half_of(lst, h):
-            return lst[:, 16 * h : 16 * (h + 1)]
+            return lst[:, HALF // 16 * h : HALF // 16 * (h + 1)]
 
-        def cols(h):
-            return slice(HALF * h, HALF * (h + 1))
+        def load_words(table, src):
+            nc.sync.dma_start(table[:].bitcast(I32), src[0].rearrange("p n t -> p (n t)").bitcast(I32))
 
         def load_scale_rows(queue, plane, src):
             for j in range(PACK):
-                queue.dma_start(plane[j:P:32, :].bitcast(I32), src[0, j:16:PACK, :].bitcast(I32))
+                queue.dma_start(plane[j:P:32, :].bitcast(I32), src[0, j:SCALE_ROWS:PACK, :].bitcast(I32))
 
-        def deal(engine_copy, dst, src):
-            engine_copy(dst.rearrange("p (t m) -> p m t", t=PACK), src.rearrange("p (m t) -> p m t", t=PACK))
+        def deal_words(copy, dst, src):
+            copy(dst.rearrange("p (t m) -> p m t", t=PACK), src.rearrange("p (m t) -> p m t", t=PACK))
 
-        def interleave(dst, src):
+        def weave(dst, src):
             nc.vector.tensor_copy(
                 dst[:].rearrange("p (c i t) -> p c t i", i=4, t=PACK),
                 src.rearrange("p t (c i) -> p c t i", i=4),
             )
+
+        def quantise(codes, scales, woven):
+            nc.vector.quantize_mx(out=codes.bitcast(FP8X4), scales=scales, in_=woven[:])
+
+        def gather(on_scalar, dst, window, lst):
+            if on_scalar:
+                nc.scalar.activation(dst, window[:].indirect(lst), ACT.Copy)
+            else:
+                nc.vector.tensor_copy(dst, window[:].indirect(lst))
 
         d_scale_table = new("d_scale_table", [P, G], U8)
         x_scale_table = new("x_scale_table", [P, T], U8)
@@ -65,165 +88,152 @@ def tile_picked_kjehqduelnorm_none_po_kernel(
             nc.vector.memset(plane[:].bitcast(I32), 0)
 
         k1_t = load_list("k1_t", k1)
-        nc.sync.dma_start(d_scale_table[:].bitcast(I32), d_scales[0].bitcast(I32).unsqueeze(1).to_broadcast([16, 8, G // 4]))
+        nc.sync.dma_start(
+            d_scale_table[:].bitcast(I32),
+            d_scales[0].bitcast(I32).unsqueeze(1).to_broadcast([SCALE_ROWS, P // SCALE_ROWS, G // 4]),
+        )
         two_t = load_list("two_t", two)
         x_word_table = new("x_word_table", [P, T], U32)
-        nc.sync.dma_start(x_word_table[:].bitcast(I32), x_words[0].rearrange("p n t -> p (n t)").bitcast(I32))
+        load_words(x_word_table, x_words)
         d_word_table = new("d_word_table", [P, G], U32)
-        nc.sync.dma_start(d_word_table[:].bitcast(I32), d_words[0].rearrange("p n t -> p (n t)").bitcast(I32))
-        offs_t = load_list("offs_t", offs)
-        n3_t = load_list("n3_t", n3)
-        n4_t = load_list("n4_t", n4)
-        n1_t = load_list("n1_t", n1)
-        n2_t = load_list("n2_t", n2)
-        n5_t = load_list("n5_t", n5)
+        load_words(d_word_table, d_words)
+        offs_t, n3_t, n4_t, n1_t, n2_t, n5_t = (
+            load_list(name, src)
+            for name, src in (("offs_t", offs), ("n3_t", n3), ("n4_t", n4), ("n1_t", n1), ("n2_t", n2), ("n5_t", n5))
+        )
         load_scale_rows(nc.scalar, x_scale_table, x_scales)
-        w_raw = []
-        for i, src in enumerate((w1_words, w2_words)):
-            w_raw.append(new("w_raw%d" % i, [P, 2 * S], U8))
-            nc.gpsimd.dma_start(w_raw[i][:].bitcast(I32), src[0].bitcast(I32))
+        w_raw = [new("w_raw%d" % i, [P, 2 * S], U8) for i in range(2)]
+        for raw, src in zip(w_raw, (w1_words, w2_words)):
+            nc.gpsimd.dma_start(raw[:].bitcast(I32), src[0].bitcast(I32))
 
         spare_in = new("spare_in", [P, 1], F32)
         nc.vector.memset(spare_in[:], 0.0)
         spare_sig = new("spare_sig", [P, 1], F32)
         nc.scalar.activation(spare_sig[:], spare_in[:], ACT.Sigmoid)
-        key_scale_picked = new("key_scale_picked", [P, S], U8)
-        nc.vector.tensor_copy(key_scale_picked[:], d_scale_table[:].indirect(k1_t[:]))
-        key_scale_dealt = new("key_scale_dealt", [P, S], U8)
-        deal(nc.vector.tensor_copy, key_scale_dealt[:], key_scale_picked[:])
-        for j in range(PACK):
-            nc.scalar.dma_start(key_scales[j:P:32, :].bitcast(I32), key_scale_dealt[8 * j : P : 32, :].bitcast(I32))
 
-        def pick(name, table, lst, dtype, tag=None):
-            picked = new(name, [P, S], dtype, tag=tag)
+        def pick(name, table, lst, dtype, reuse=None):
+            picked = new(name, [P, S], dtype, reuse)
             nc.vector.tensor_copy(picked[:], table[:].indirect(lst[:]))
             return picked
 
+        key_scale_picked = pick("key_scale_picked", d_scale_table, k1_t, U8)
+        key_scale_dealt = new("key_scale_dealt", [P, S], U8)
+        nc.vector.tensor_copy(
+            key_scale_dealt[:].rearrange("p (t m) -> p t m", t=PACK),
+            key_scale_picked[:].rearrange("p (m t) -> p t m", t=PACK),
+        )
+        for j in range(PACK):
+            nc.scalar.dma_start(key_scales[j:P:32, :].bitcast(I32), key_scale_dealt[8 * j : P : 32, :].bitcast(I32))
+
         tok_b_words = pick("tok_b_words", x_word_table, two_t, U32)
-
-        key_picked = new("key_picked", [P, S], U32)
-        nc.vector.tensor_copy(key_picked[:], d_word_table[:].indirect(k1_t[:]))
+        key_picked = pick("key_picked", d_word_table, k1_t, U32)
         key_words = new("key_words", [P, S], U32)
-        deal(nc.vector.tensor_copy, key_words[:], key_picked[:])
-        tok_b = (tok_b_words, pick("tok_b_scales", x_scale_table, two_t, U8))
+        deal_words(nc.vector.tensor_copy, key_words[:], key_picked[:])
+        tok_b_scales = pick("tok_b_scales", x_scale_table, two_t, U8)
 
-        w_scale_raw = new("w_scale_raw", [P, 2 * S], U8, tag="d_word_table")
+        w_scale_raw = new("w_scale_raw", [P, 2 * S], U8, reuse="d_word_table")
         nc.gpsimd.memset(w_scale_raw[:].bitcast(I32), 0)
         load_scale_rows(nc.sync, w_scale_raw[:, 0:S], w1_scales)
         load_scale_rows(nc.sync, w_scale_raw[:, S : 2 * S], w2_scales)
 
-        def score(tag, tok):
-            banks = []
-            for t in range(PACK):
-                bank = ps.tile([P, S], F32, name="%s%d" % (tag, t), tag="%s%d" % (tag, t))
+        def score(name, words, scales):
+            banks = [psum.tile([P, S], F32, name="%s%d" % (name, t), tag="%s%d" % (name, t)) for t in tiles]
+            for t in tiles:
                 nc.tensor.matmul_mx(
-                    out=bank[:], lhsT=key_words[:, P * t : P * (t + 1)].bitcast(FP8X4),
+                    out=banks[t][:], lhsT=key_words[:, P * t : P * (t + 1)].bitcast(FP8X4),
                     lhsT_scale=key_scales[:, P * t : P * (t + 1)],
-                    rhs=tok[0][:].bitcast(FP8X4), rhs_scale=tok[1][:], start=True, stop=True,
+                    rhs=words[:].bitcast(FP8X4), rhs_scale=scales[:], start=True, stop=True,
                 )
-                banks.append(bank)
             return banks
 
-        b_bank = score("pb", tok_b)
-        tok_a = (pick("tok_a_words", x_word_table, offs_t, U32, tag="key_picked"), pick("tok_a_scales", x_scale_table, offs_t, U8, tag="key_scale_picked"))
-        a_bank = score("pa", tok_a)
+        b_bank = score("b_bank", tok_b_words, tok_b_scales)
+        tok_a_words = pick("tok_a_words", x_word_table, offs_t, U32, reuse="key_picked")
+        tok_a_scales = pick("tok_a_scales", x_scale_table, offs_t, U8, reuse="key_scale_picked")
+        a_bank = score("a_bank", tok_a_words, tok_a_scales)
 
-        rows = {}
-        for name, src, tag in (("gm", gm, "tok_b_words"), ("sl", sl, "tok_b_scales"), ("th", th, "x_word_table"), ("gn", gn, "x_scale_table")):
-            rows[name] = new(name + "_t", [P, PACK], F32, tag=tag)
-            nc.sync.dma_start(rows[name][:], src.rearrange("(p t) o -> p (t o)", t=PACK))
-        w_words = []
-        for i in range(2):
-            w_words.append(new("w_words%d" % i, [P, 2 * S], U8))
-            deal(nc.scalar.copy, w_words[i][:].bitcast(U16), w_raw[i][:].bitcast(U16))
+        def load_rows(name, src, reuse):
+            rows = new(name, [P, PACK], F32, reuse)
+            nc.sync.dma_start(rows[:], src.rearrange("(p t) o -> p (t o)", t=PACK))
+            return rows
 
-        sig_bias = new("sig_bias", [P, PACK], F32)
-        gn16 = new("gn16", [P, PACK], F32)
+        gm_t = load_rows("gm_t", gm, "tok_b_words")
+        sl_t = load_rows("sl_t", sl, "tok_b_scales")
+        th_t = load_rows("th_t", th, "x_word_table")
+        gn_t = load_rows("gn_t", gn, "x_scale_table")
+        w_words = [new("w_words%d" % i, [P, 2 * S], U8) for i in range(2)]
+        for dealt, raw in zip(w_words, w_raw):
+            deal_words(nc.scalar.copy, dealt[:].bitcast(U16), raw[:].bitcast(U16))
 
-        def row_constants():
-            nc.vector.scalar_tensor_tensor(sig_bias[:], rows["sl"][:], -1.0, rows["th"][:], ALU.mult, ALU.mult)
-            nc.vector.tensor_scalar(gn16[:], rows["gn"][:], 0.0625, None, ALU.mult)
-
-        def gather(on_scalar, dst, window, lst):
-            if on_scalar:
-                nc.scalar.activation(dst, window[:].indirect(lst), ACT.Copy)
-            else:
-                nc.vector.tensor_copy(dst, window[:].indirect(lst))
-
-        def per_tile(name, width, dtype=F32):
-            return [new("%s%d" % (name, t), [P, width], dtype) for t in range(PACK)]
-
-        b_win, a_win, st_win, dt_win = (per_tile(n, S) for n in ("b_win", "a_win", "st_win", "dt_win"))
-        pa, pb, diff, sa, sbm, ra, rb = (per_tile(n, HALF) for n in ("pa_", "pb_", "diff", "sa", "sbm", "ra", "rb"))
-        a_n1 = per_tile("a_n1", S)
-        z2_planes = new("z2_planes", [P, PACK, S], BF16)
-
-        def evac_b(t):
-            nc.scalar.activation(b_win[t][:], b_bank[t][:], ACT.Copy, scale=0.0625)
-
-        def evac_a(t):
-            nc.scalar.activation(a_win[t][:], a_bank[t][:], ACT.Copy, scale=0.0625)
-
-        def evac_a_vector(t):
-            nc.vector.tensor_scalar(a_win[t][:], a_bank[t][:], 0.0625, None, ALU.mult)
-
-        def fetch_pairs(t, on_scalar):
-            gather(on_scalar, pa[t][:], b_win[t], n3_t[:])
-            gather(on_scalar, pb[t][:], b_win[t], n4_t[:])
-
-        def differ(t):
+        b_win, dt_win = per_tile("b_win", S), per_tile("dt_win", S)
+        pa, pb, diff = per_tile("pa", HALF), per_tile("pb", HALF), per_tile("diff", HALF)
+        win_a, win_b = per_tile("win_a", HALF), per_tile("win_b", HALF)
+        for t in tiles:
+            nc.scalar.activation(b_win[t][:], b_bank[t][:], ACT.Copy, scale=SCORE)
+            gather(t not in PAIRS_ON_VECTOR, pa[t][:], b_win[t], n3_t[:])
+            gather(t not in PAIRS_ON_VECTOR, pb[t][:], b_win[t], n4_t[:])
             nc.vector.tensor_tensor(diff[t][:], pa[t][:], pb[t][:], ALU.subtract)
 
-        def differ_g(t):
-            nc.gpsimd.tensor_tensor(diff[t][:], pa[t][:], pb[t][:], ALU.subtract)
+        sides = ((n3_t, pa, win_a), (n4_t, pb, win_b))
+        on_vector = [t for t in tiles if t != SCATTER_ON_SCALAR]
+        first = on_vector[0]
+        for t in [first, SCATTER_ON_SCALAR] + on_vector[1:]:
+            nc.scalar.activation(win_a[t][:], diff[t][:], ACT.Sigmoid)
+            nc.scalar.activation(win_b[t][:], diff[t][:], ACT.Sigmoid, scale=-1.0)
 
-        def product_g(t, side):
-            r_, p_, s_ = ((ra, pa, sa), (rb, pb, sbm))[side]
-            nc.gpsimd.tensor_tensor(r_[t][:], p_[t][:], s_[t][:], ALU.mult)
+        def scatter_product(t, side):
+            lst, value, win = sides[side]
+            nc.vector.tensor_tensor(dt_win[t][:].indirect(lst[:]), value[t][:], win[t][:], ALU.mult)
 
-        def put_copy(t, side):
-            lst, r_ = ((n3_t, ra), (n4_t, rb))[side]
-            nc.vector.tensor_copy(dt_win[t][:].indirect(lst[:]), r_[t][:])
+        scatter_product(first, 0)
+        product = [new("product%d" % side, [P, HALF], F32) for side in range(2)]
+        for side, (lst, value, win) in enumerate(sides):
+            nc.vector.tensor_tensor(product[side][:], value[SCATTER_ON_SCALAR][:], win[SCATTER_ON_SCALAR][:], ALU.mult)
+        scatter_product(first, 1)
+        for t in on_vector[1:]:
+            scatter_product(t, 0)
+            scatter_product(t, 1)
 
-        def regroup_scalar(t):
-            nc.scalar.activation(z2_planes[:, t, :], dt_win[t][:], ACT.Copy, scale=rows["gm"][:, t : t + 1])
+        a_win, a_n1, st_win = per_tile("a_win", S), per_tile("a_n1_", S), per_tile("st_win", S)
+        z2_planes = new("z2_planes", [P, PACK, S], BF16)
 
-        def regroup_g(t):
-            nc.gpsimd.tensor_scalar(z2_planes[:, t, :], dt_win[t][:], rows["gm"][:, t : t + 1], 0.0, ALU.mult, ALU.add)
+        def copy_a(t):
+            nc.scalar.activation(a_win[t][:], a_bank[t][:], ACT.Copy, scale=SCORE)
 
-        def duel(t):
-            nc.scalar.activation(sa[t][:], diff[t][:], ACT.Sigmoid)
-            nc.scalar.activation(sbm[t][:], diff[t][:], ACT.Sigmoid, scale=-1.0)
+        def fetch_n1(t):
+            for h in halves:
+                gather(True, a_n1[t][:, cols(h)], a_win[t], half_of(n1_t, h))
 
-        def put_vector(t, side):
-            lst, p_, s_ = ((n3_t, pa, sa), (n4_t, pb, sbm))[side]
-            nc.vector.tensor_tensor(dt_win[t][:].indirect(lst[:]), p_[t][:], s_[t][:], ALU.mult)
+        def scatter_copy(side):
+            nc.scalar.activation(dt_win[SCATTER_ON_SCALAR][:].indirect(sides[side][0][:]), product[side][:], ACT.Copy)
 
-        def products(t):
-            nc.vector.tensor_tensor(ra[t][:], pa[t][:], sa[t][:], ALU.mult)
-            nc.vector.tensor_tensor(rb[t][:], pb[t][:], sbm[t][:], ALU.mult)
+        copy_a(0)
+        fetch_n1(0)
+        scatter_copy(0)
+        copy_a(1)
+        scatter_copy(1)
+        nc.scalar.activation(
+            z2_planes[:, SCATTER_ON_SCALAR, :], dt_win[SCATTER_ON_SCALAR][:], ACT.Copy,
+            scale=gm_t[:, SCATTER_ON_SCALAR : SCATTER_ON_SCALAR + 1],
+        )
+        fetch_n1(1)
+        for t in (2, 3):
+            copy_a(t)
+            fetch_n1(t)
 
-        def put_scalar(t, side):
-            lst, r_ = ((n3_t, ra), (n4_t, rb))[side]
-            nc.scalar.activation(dt_win[t][:].indirect(lst[:]), r_[t][:], ACT.Copy)
-
-        def regroup(t):
-            nc.vector.tensor_scalar(z2_planes[:, t, :], dt_win[t][:], rows["gm"][:, t : t + 1], None, ALU.mult)
-
-        def fetch_n1(t, on_scalar):
-            for h in range(2):
-                gather(on_scalar, a_n1[t][:, cols(h)], a_win[t], half_of(n1_t, h))
-
-        def step(t):
-            nc.vector.scalar_tensor_tensor(st_win[t][:], a_bank[t][:], 0.0625, a_n1[t][:], ALU.mult, ALU.subtract)
+        for t in on_vector:
+            nc.vector.tensor_scalar(z2_planes[:, t, :], dt_win[t][:], gm_t[:, t : t + 1], None, ALU.mult)
 
         w_scales = new("w_scales", [P, 2 * S], U8)
-
-        def deal_w_scales():
-            nc.vector.tensor_copy(
-                w_scales[:].rearrange("p (w t m) -> p w m t", w=2, t=PACK),
-                w_scale_raw[:].rearrange("p (w m t) -> p w m t", w=2, t=PACK),
-            )
+        nc.vector.tensor_copy(
+            w_scales[:].rearrange("p (w t m) -> p w t m", w=2, t=PACK),
+            w_scale_raw[:].rearrange("p (w m t) -> p w t m", w=2, t=PACK),
+        )
+        gate_bias = new("gate_bias", [P, PACK], F32)
+        nc.vector.scalar_tensor_tensor(gate_bias[:], sl_t[:], -1.0, th_t[:], ALU.mult, ALU.mult)
+        gn_score = new("gn_score", [P, PACK], F32)
+        nc.vector.tensor_scalar(gn_score[:], gn_t[:], SCORE, None, ALU.mult)
+        for t in tiles:
+            nc.vector.scalar_tensor_tensor(st_win[t][:], a_bank[t][:], SCORE, a_n1[t][:], ALU.mult, ALU.subtract)
 
         def w_pass(bank, i, t, codes, scales, start, stop):
             nc.tensor.matmul_mx(
@@ -232,200 +242,68 @@ def tile_picked_kjehqduelnorm_none_po_kernel(
                 rhs=codes.bitcast(FP8X4), rhs_scale=scales, start=start, stop=stop,
             )
 
-        h_bank = [[], []]
-        z2_packed = [new("z2_packed%d" % h, [P, PACK * HALF], BF16, tag="a_n1%d" % (2 + h)) for h in range(2)]
         z2_codes = new("z2_codes", [P, S], U32)
         z2_scales = new("z2_scales", [P, S], U8)
-
-        def pack_z2(h):
-            interleave(z2_packed[h], z2_planes[:, :, cols(h)])
-
-        def quant_z2(h):
-            nc.vector.quantize_mx(out=z2_codes[:, cols(h)].bitcast(FP8X4), scales=z2_scales[:, cols(h)], in_=z2_packed[h][:])
-
-        sg = [new("sg%d" % h, [P, PACK, HALF], F32) for h in range(2)]
-        z_planes = [new("z_planes%d" % h, [P, PACK, HALF], BF16) for h in range(2)]
-        z_packed = [new("z_packed%d" % h, [P, PACK * HALF], BF16) for h in range(2)]
-
-        z_codes = [new("z_codes%d" % h, [P, HALF], U32) for h in range(2)]
-        z_scales = [new("z_scales%d" % h, [P, HALF], U8) for h in range(2)]
-        r_win = [new("r_win%d" % t, [P, S], F32, tag=tag) for t, tag in enumerate(("z_packed1", "z_codes1", "z_scales1", "z2_codes"))]
-
-        def gate(h, t):
-            nc.scalar.activation(
-                sg[h][:, t, :], st_win[t][:].indirect(half_of(n2_t, h)), ACT.Sigmoid,
-                bias=sig_bias[:, t : t + 1], scale=rows["sl"][:, t : t + 1],
-            )
-
-        def gated(h, t):
-            nc.vector.scalar_tensor_tensor(
-                z_planes[h][:, t, :], a_bank[t][:, cols(h)], gn16[:, t : t + 1], sg[h][:, t, :], ALU.mult, ALU.mult
-            )
-
-        def pack_z(h):
-            interleave(z_packed[h], z_planes[h][:])
-
-        def quant_z(h):
-            nc.vector.quantize_mx(out=z_codes[h][:].bitcast(FP8X4), scales=z_scales[h][:], in_=z_packed[h][:])
-            for t in range(PACK):
-                h_bank[h].append(ps.tile([P, S], F32, name="ph%d_%d" % (h, t), tag=("pb%d", "pa%d")[h] % t)[:, 0:HALF])
+        h_bank = []
+        for h in halves:
+            z2_woven = new("z2_woven%d" % h, [P, PACK * HALF], BF16, reuse="a_n1_%d" % (2 + h))
+            weave(z2_woven, z2_planes[:, :, cols(h)])
+            quantise(z2_codes[:, cols(h)], z2_scales[:, cols(h)], z2_woven)
+            sg = new("sg%d" % h, [P, PACK, HALF], F32)
+            z_planes = new("z_planes%d" % h, [P, PACK, HALF], BF16)
+            for t in tiles:
+                nc.scalar.activation(
+                    sg[:, t, :], st_win[t][:].indirect(half_of(n2_t, h)), ACT.Sigmoid,
+                    bias=gate_bias[:, t : t + 1], scale=sl_t[:, t : t + 1],
+                )
+                nc.vector.scalar_tensor_tensor(
+                    z_planes[:, t, :], a_bank[t][:, cols(h)], gn_score[:, t : t + 1], sg[:, t, :], ALU.mult, ALU.mult
+                )
+            z_woven = new("z_woven%d" % h, [P, PACK * HALF], BF16)
+            weave(z_woven, z_planes[:])
+            z_codes = new("z_codes%d" % h, [P, HALF], U32)
+            z_scales = new("z_scales%d" % h, [P, HALF], U8)
+            quantise(z_codes[:], z_scales[:], z_woven)
+            h_bank.append([])
+            for t in tiles:
+                bank = psum.tile([P, S], F32, name="h_bank%d_%d" % (h, t), tag=("b_bank%d", "a_bank%d")[h] % t)
+                h_bank[h].append(bank[:, 0:HALF])
                 w_pass(h_bank[h][t], 1, t, z2_codes[:, cols(h)], z2_scales[:, cols(h)], True, False)
-                w_pass(h_bank[h][t], 0, t, z_codes[h][:], z_scales[h][:], False, True)
+                w_pass(h_bank[h][t], 0, t, z_codes[:], z_scales[:], False, True)
 
-        size = [[new("size%d_%d" % (h, t), [P, HALF], F32, tag="size%d_%d" % (h, t % 2)) for t in range(PACK)] for h in range(2)]
+        spare_root = new("spare_root", [P, 1], F32)
+        nc.scalar.activation(spare_root[:], sg[:, PACK - 1, 0:1], ACT.Abs_reciprocal_sqrt, bias=0.5)
+
+        r_win = [
+            new("r_win%d" % t, [P, S], F32, reuse)
+            for t, reuse in enumerate(("z_woven1", "z_codes1", "z_scales1", "z2_codes"))
+        ]
         root = per_tile("root", S)
-
-        def warm_root():
-            spare_root = new("spare_root", [P, 1], F32)
-            nc.scalar.activation(spare_root[:], sg[1][:, PACK - 1, 0:1], ACT.Abs_reciprocal_sqrt, bias=0.5)
-
-        def absolute(h, t):
-            nc.scalar.activation(size[h][t][:], h_bank[h][t], ACT.Abs)
-
-        def inverse_root(h, t):
-            nc.scalar.activation(root[t][:, cols(h)], size[h][t][:], ACT.Abs_reciprocal_sqrt, bias=0.5)
-
-        def square(t, c, engine):
-            engine.tensor_tensor(r_win[t][:, c], root[t][:, c], root[t][:, c], ALU.mult)
+        for h in halves:
+            for t in tiles:
+                size = new("size%d_%d" % (h, t), [P, HALF], F32, reuse="size%d_%d" % (h, t % 2))
+                nc.scalar.activation(size[:], h_bank[h][t], ACT.Abs)
+                nc.scalar.activation(root[t][:, cols(h)], size[:], ACT.Abs_reciprocal_sqrt, bias=0.5)
+                if h == 1 and t in LATE_TILES:
+                    nc.scalar.activation(r_win[t][:, cols(h)], root[t][:, cols(h)], ACT.Square)
+                else:
+                    nc.vector.tensor_tensor(r_win[t][:, cols(h)], root[t][:, cols(h)], root[t][:, cols(h)], ALU.mult)
 
         out_rows = out_0.rearrange("(p t) j -> p t j", t=PACK)
+        out_words = out_1[0].rearrange("p n t -> p (n t)").bitcast(I32)
         y_codes = new("y_codes", [P, S], U32)
         y_scales = new("y_scales", [P, S], U8)
-        code_rows = out_1[0].rearrange("p n t -> p (n t)").bitcast(I32)
-        r_n5 = [new("r_n5_%d" % h, [P, PACK, HALF], F32) for h in range(2)]
-        y = [new("y%d" % h, [P, PACK, HALF], F32) for h in range(2)]
-        y_packed = [new("y_packed%d" % h, [P, PACK * HALF], BF16) for h in range(2)]
-
-        def fetch_n5(h, t, on_scalar):
-            gather(on_scalar, r_n5[h][:, t, :], r_win[t], half_of(n5_t, h))
-
-        def result(h, t):
-            nc.vector.tensor_tensor(y[h][:, t, :], h_bank[h][t], r_n5[h][:, t, :], ALU.mult)
-
-        def store_y(h):
-            nc.sync.dma_start(out_rows[:, :, cols(h)], y[h][:])
-
-        def pack_y(h):
-            interleave(y_packed[h], y[h][:])
-
-        def quant_y(h):
-            nc.vector.quantize_mx(out=y_codes[:, cols(h)].bitcast(FP8X4), scales=y_scales[:, cols(h)], in_=y_packed[h][:])
-            nc.sync.dma_start(code_rows[:, cols(h)], y_codes[:, cols(h)].bitcast(I32))
-
-        evac_b(0)
-        fetch_pairs(0, True)
-        evac_b(1)
-        evac_b(2)
-        differ(0)
-        fetch_pairs(1, False)
-        evac_b(3)
-        fetch_pairs(3, True)
-        differ(1)
-        fetch_pairs(2, False)
-        duel(1)
-        differ(3)
-        differ(2)
-        duel(0)
-        put_vector(1, 0)
-        products(0)
-        duel(2)
-        duel(3)
-        put_vector(1, 1)
-        evac_a(0)
-        fetch_n1(0, True)
-        put_vector(2, 0)
-        put_scalar(0, 0)
-        evac_a(1)
-        put_vector(2, 1)
-        put_scalar(0, 1)
-        regroup_scalar(0)
-        put_vector(3, 0)
-        fetch_n1(1, True)
-        regroup(1)
-        regroup(2)
-        put_vector(3, 1)
-        evac_a(2)
-        fetch_n1(2, True)
-        step(0)
-        step(1)
-        deal_w_scales()
-        row_constants()
-        regroup(3)
-        evac_a(3)
-        fetch_n1(3, True)
-        step(2)
-        step(3)
-        pack_z2(0)
-        gate(0, 0)
-        gate(0, 1)
-        gate(0, 2)
-        gate(0, 3)
-        gated(0, 0)
-        quant_z2(0)
-        gated(0, 1)
-        gated(0, 2)
-        gated(0, 3)
-        gate(1, 0)
-        pack_z(0)
-        gate(1, 1)
-        gated(1, 0)
-        quant_z(0)
-        pack_z2(1)
-        gate(1, 2)
-        gated(1, 1)
-        quant_z2(1)
-        gate(1, 3)
-        warm_root()
-        gated(1, 2)
-        gated(1, 3)
-        pack_z(1)
-        quant_z(1)
-        absolute(0, 0)
-        inverse_root(0, 0)
-        square(0, cols(0), nc.vector)
-        absolute(0, 1)
-        inverse_root(0, 1)
-        square(1, cols(0), nc.vector)
-        absolute(0, 2)
-        inverse_root(0, 2)
-        square(2, cols(0), nc.vector)
-        absolute(0, 3)
-        inverse_root(0, 3)
-        square(3, cols(0), nc.vector)
-        absolute(1, 0)
-        inverse_root(1, 0)
-        square(0, cols(1), nc.vector)
-        absolute(1, 1)
-        inverse_root(1, 1)
-        fetch_n5(0, 0, False)
-        square(1, cols(1), nc.vector)
-        absolute(1, 2)
-        inverse_root(1, 2)
-        result(0, 0)
-        square(2, cols(1), nc.vector)
-        absolute(1, 3)
-        inverse_root(1, 3)
-        fetch_n5(0, 1, False)
-        square(3, cols(1), nc.vector)
-        fetch_n5(0, 2, True)
-        result(0, 1)
-        fetch_n5(0, 3, True)
-        result(0, 2)
-        fetch_n5(1, 0, True)
-        result(0, 3)
-        store_y(0)
-        pack_y(0)
-        fetch_n5(1, 1, True)
-        result(1, 0)
-        quant_y(0)
-        fetch_n5(1, 2, True)
-        result(1, 1)
-        fetch_n5(1, 3, True)
-        result(1, 2)
-        result(1, 3)
-        store_y(1)
-        pack_y(1)
-        quant_y(1)
+        for h in halves:
+            r_n5 = new("r_n5_%d" % h, [P, PACK, HALF], F32)
+            y = new("y%d" % h, [P, PACK, HALF], F32)
+            for t in tiles:
+                gather(h == 1 or t in LATE_TILES, r_n5[:, t, :], r_win[t], half_of(n5_t, h))
+                nc.vector.tensor_tensor(y[:, t, :], h_bank[h][t], r_n5[:, t, :], ALU.mult)
+            nc.sync.dma_start(out_rows[:, :, cols(h)], y[:])
+            y_woven = new("y_woven%d" % h, [P, PACK * HALF], BF16)
+            weave(y_woven, y[:])
+            quantise(y_codes[:, cols(h)], y_scales[:, cols(h)], y_woven)
+            nc.sync.dma_start(out_words[:, cols(h)], y_codes[:, cols(h)].bitcast(I32))
         for j in range(PACK):
             queue = nc.scalar if j % 2 else nc.sync
-            queue.dma_start(out_2[0, j:16:PACK, :].bitcast(I32), y_scales[j:P:32, :].bitcast(I32))
+            queue.dma_start(out_2[0, j:SCALE_ROWS:PACK, :].bitcast(I32), y_scales[j:P:32, :].bitcast(I32))

from contextlib import ExitStack

import concourse.mybir as mybir

F32 = mybir.dt.float32
BF16 = mybir.dt.bfloat16
I32 = mybir.dt.int32
U32 = mybir.dt.uint32
U16 = mybir.dt.uint16
U8 = mybir.dt.uint8
FP8X4 = mybir.dt.float8_e4m3fn_x4
FP4X4 = mybir.dt.float4_e2m1fn_x4
ALU = mybir.AluOpType
ACT = mybir.ActivationFunctionType

P = 128
PACK = 4
S = 512
HALF = S // 2
T = 1024
G = 2048
SCALE_ROWS = 16
SCORE = 0.0625
FLOPS = 4 * 2 * 512 * 512 * 512

PAIRS_ON_VECTOR = (1, 2)
SCATTER_ON_SCALAR = 0
LATE_TILES = (2, 3)


def tile_picked_kjehqduelnorm_none_po_kernel(
    tc, x_words, x_scales, d_words, d_scales, sl, th, gn, gm, w1_words, w1_scales, w2_words, w2_scales,
    offs, k1, two, n1, n2, n3, n4, n5, out_0, out_1, out_2,
):
    nc = tc.nc
    tiles = range(PACK)
    halves = range(2)
    with ExitStack() as ctx:
        sbuf = ctx.enter_context(tc.tile_pool(name="sbuf", bufs=1))
        psum = ctx.enter_context(tc.psum_pool(name="psum", bufs=1))

        def new(name, shape, dtype, reuse=None):
            return sbuf.tile(shape, dtype, name=name, tag=reuse or name, align_bytes=64)

        def per_tile(name, width):
            return [new("%s%d" % (name, t), [P, width], F32) for t in tiles]

        def cols(h):
            return slice(HALF * h, HALF * (h + 1))

        def load_list(name, src):
            lst = new(name, list(src.shape), U16)
            nc.sync.dma_start(lst[:], src)
            return lst

        def half_of(lst, h):
            return lst[:, HALF // 16 * h : HALF // 16 * (h + 1)]

        def load_words(table, src):
            nc.sync.dma_start(table[:].bitcast(I32), src[0].rearrange("p n t -> p (n t)").bitcast(I32))

        def load_scale_rows(queue, plane, src):
            for j in range(PACK):
                queue.dma_start(plane[j:P:32, :].bitcast(I32), src[0, j:SCALE_ROWS:PACK, :].bitcast(I32))

        def deal_words(copy, dst, src):
            copy(dst.rearrange("p (t m) -> p m t", t=PACK), src.rearrange("p (m t) -> p m t", t=PACK))

        def weave(dst, src):
            nc.vector.tensor_copy(
                dst[:].rearrange("p (c i t) -> p c t i", i=4, t=PACK),
                src.rearrange("p t (c i) -> p c t i", i=4),
            )

        def quantise(codes, scales, woven):
            nc.vector.quantize_mx(out=codes.bitcast(FP8X4), scales=scales, in_=woven[:])

        def gather(on_scalar, dst, window, lst):
            if on_scalar:
                nc.scalar.activation(dst, window[:].indirect(lst), ACT.Copy)
            else:
                nc.vector.tensor_copy(dst, window[:].indirect(lst))

        d_scale_table = new("d_scale_table", [P, G], U8)
        x_scale_table = new("x_scale_table", [P, T], U8)
        key_scales = new("key_scales", [P, S], U8)
        for plane in (x_scale_table, key_scales):
            nc.vector.memset(plane[:].bitcast(I32), 0)

        k1_t = load_list("k1_t", k1)
        nc.sync.dma_start(
            d_scale_table[:].bitcast(I32),
            d_scales[0].bitcast(I32).unsqueeze(1).to_broadcast([SCALE_ROWS, P // SCALE_ROWS, G // 4]),
        )
        two_t = load_list("two_t", two)
        x_word_table = new("x_word_table", [P, T], U32)
        load_words(x_word_table, x_words)
        d_word_table = new("d_word_table", [P, G], U32)
        load_words(d_word_table, d_words)
        offs_t, n3_t, n4_t, n1_t, n2_t, n5_t = (
            load_list(name, src)
            for name, src in (("offs_t", offs), ("n3_t", n3), ("n4_t", n4), ("n1_t", n1), ("n2_t", n2), ("n5_t", n5))
        )
        load_scale_rows(nc.scalar, x_scale_table, x_scales)
        w_raw = [new("w_raw%d" % i, [P, 2 * S], U8) for i in range(2)]
        for raw, src in zip(w_raw, (w1_words, w2_words)):
            nc.gpsimd.dma_start(raw[:].bitcast(I32), src[0].bitcast(I32))

        spare_in = new("spare_in", [P, 1], F32)
        nc.vector.memset(spare_in[:], 0.0)
        spare_sig = new("spare_sig", [P, 1], F32)
        nc.scalar.activation(spare_sig[:], spare_in[:], ACT.Sigmoid)

        def pick(name, table, lst, dtype, reuse=None):
            picked = new(name, [P, S], dtype, reuse)
            nc.vector.tensor_copy(picked[:], table[:].indirect(lst[:]))
            return picked

        key_scale_picked = pick("key_scale_picked", d_scale_table, k1_t, U8)
        key_scale_dealt = new("key_scale_dealt", [P, S], U8)
        nc.vector.tensor_copy(
            key_scale_dealt[:].rearrange("p (t m) -> p t m", t=PACK),
            key_scale_picked[:].rearrange("p (m t) -> p t m", t=PACK),
        )
        for j in range(PACK):
            nc.scalar.dma_start(key_scales[j:P:32, :].bitcast(I32), key_scale_dealt[8 * j : P : 32, :].bitcast(I32))

        tok_b_words = pick("tok_b_words", x_word_table, two_t, U32)
        key_picked = pick("key_picked", d_word_table, k1_t, U32)
        key_words = new("key_words", [P, S], U32)
        deal_words(nc.vector.tensor_copy, key_words[:], key_picked[:])
        tok_b_scales = pick("tok_b_scales", x_scale_table, two_t, U8)

        w_scale_raw = new("w_scale_raw", [P, 2 * S], U8, reuse="d_word_table")
        nc.gpsimd.memset(w_scale_raw[:].bitcast(I32), 0)
        load_scale_rows(nc.sync, w_scale_raw[:, 0:S], w1_scales)
        load_scale_rows(nc.sync, w_scale_raw[:, S : 2 * S], w2_scales)

        def score(name, words, scales):
            banks = [psum.tile([P, S], F32, name="%s%d" % (name, t), tag="%s%d" % (name, t)) for t in tiles]
            for t in tiles:
                nc.tensor.matmul_mx(
                    out=banks[t][:], lhsT=key_words[:, P * t : P * (t + 1)].bitcast(FP8X4),
                    lhsT_scale=key_scales[:, P * t : P * (t + 1)],
                    rhs=words[:].bitcast(FP8X4), rhs_scale=scales[:], start=True, stop=True,
                )
            return banks

        b_bank = score("b_bank", tok_b_words, tok_b_scales)
        tok_a_words = pick("tok_a_words", x_word_table, offs_t, U32, reuse="key_picked")
        tok_a_scales = pick("tok_a_scales", x_scale_table, offs_t, U8, reuse="key_scale_picked")
        a_bank = score("a_bank", tok_a_words, tok_a_scales)

        def load_rows(name, src, reuse):
            rows = new(name, [P, PACK], F32, reuse)
            nc.sync.dma_start(rows[:], src.rearrange("(p t) o -> p (t o)", t=PACK))
            return rows

        gm_t = load_rows("gm_t", gm, "tok_b_words")
        sl_t = load_rows("sl_t", sl, "tok_b_scales")
        th_t = load_rows("th_t", th, "x_word_table")
        gn_t = load_rows("gn_t", gn, "x_scale_table")
        w_words = [new("w_words%d" % i, [P, 2 * S], U8) for i in range(2)]
        for dealt, raw in zip(w_words, w_raw):
            deal_words(nc.scalar.copy, dealt[:].bitcast(U16), raw[:].bitcast(U16))

        b_win, dt_win = per_tile("b_win", S), per_tile("dt_win", S)
        pa, pb, diff = per_tile("pa", HALF), per_tile("pb", HALF), per_tile("diff", HALF)
        win_a, win_b = per_tile("win_a", HALF), per_tile("win_b", HALF)
        for t in tiles:
            nc.scalar.activation(b_win[t][:], b_bank[t][:], ACT.Copy, scale=SCORE)
            gather(t not in PAIRS_ON_VECTOR, pa[t][:], b_win[t], n3_t[:])
            gather(t not in PAIRS_ON_VECTOR, pb[t][:], b_win[t], n4_t[:])
            nc.vector.tensor_tensor(diff[t][:], pa[t][:], pb[t][:], ALU.subtract)

        sides = ((n3_t, pa, win_a), (n4_t, pb, win_b))
        on_vector = [t for t in tiles if t != SCATTER_ON_SCALAR]
        first = on_vector[0]
        for t in [first, SCATTER_ON_SCALAR] + on_vector[1:]:
            nc.scalar.activation(win_a[t][:], diff[t][:], ACT.Sigmoid)
            nc.scalar.activation(win_b[t][:], diff[t][:], ACT.Sigmoid, scale=-1.0)

        def scatter_product(t, side):
            lst, value, win = sides[side]
            nc.vector.tensor_tensor(dt_win[t][:].indirect(lst[:]), value[t][:], win[t][:], ALU.mult)

        scatter_product(first, 0)
        product = [new("product%d" % side, [P, HALF], F32) for side in range(2)]
        for side, (lst, value, win) in enumerate(sides):
            nc.vector.tensor_tensor(product[side][:], value[SCATTER_ON_SCALAR][:], win[SCATTER_ON_SCALAR][:], ALU.mult)
        scatter_product(first, 1)
        for t in on_vector[1:]:
            scatter_product(t, 0)
            scatter_product(t, 1)

        a_win, a_n1, st_win = per_tile("a_win", S), per_tile("a_n1_", S), per_tile("st_win", S)
        z2_planes = new("z2_planes", [P, PACK, S], BF16)

        def copy_a(t):
            nc.scalar.activation(a_win[t][:], a_bank[t][:], ACT.Copy, scale=SCORE)

        def fetch_n1(t):
            for h in halves:
                gather(True, a_n1[t][:, cols(h)], a_win[t], half_of(n1_t, h))

        def scatter_copy(side):
            nc.scalar.activation(dt_win[SCATTER_ON_SCALAR][:].indirect(sides[side][0][:]), product[side][:], ACT.Copy)

        copy_a(0)
        fetch_n1(0)
        scatter_copy(0)
        copy_a(1)
        scatter_copy(1)
        nc.scalar.activation(
            z2_planes[:, SCATTER_ON_SCALAR, :], dt_win[SCATTER_ON_SCALAR][:], ACT.Copy,
            scale=gm_t[:, SCATTER_ON_SCALAR : SCATTER_ON_SCALAR + 1],
        )
        fetch_n1(1)
        for t in (2, 3):
            copy_a(t)
            fetch_n1(t)

        for t in on_vector:
            nc.vector.tensor_scalar(z2_planes[:, t, :], dt_win[t][:], gm_t[:, t : t + 1], None, ALU.mult)

        w_scales = new("w_scales", [P, 2 * S], U8)
        nc.vector.tensor_copy(
            w_scales[:].rearrange("p (w t m) -> p w t m", w=2, t=PACK),
            w_scale_raw[:].rearrange("p (w m t) -> p w t m", w=2, t=PACK),
        )
        gate_bias = new("gate_bias", [P, PACK], F32)
        nc.vector.scalar_tensor_tensor(gate_bias[:], sl_t[:], -1.0, th_t[:], ALU.mult, ALU.mult)
        gn_score = new("gn_score", [P, PACK], F32)
        nc.vector.tensor_scalar(gn_score[:], gn_t[:], SCORE, None, ALU.mult)
        for t in tiles:
            nc.vector.scalar_tensor_tensor(st_win[t][:], a_bank[t][:], SCORE, a_n1[t][:], ALU.mult, ALU.subtract)

        def w_pass(bank, i, t, codes, scales, start, stop):
            nc.tensor.matmul_mx(
                out=bank, lhsT=w_words[i][:, 2 * P * t : 2 * P * (t + 1)].bitcast(FP4X4),
                lhsT_scale=w_scales[:, S * i + P * t : S * i + P * (t + 1)],
                rhs=codes.bitcast(FP8X4), rhs_scale=scales, start=start, stop=stop,
            )

        z2_codes = new("z2_codes", [P, S], U32)
        z2_scales = new("z2_scales", [P, S], U8)
        h_bank = []
        for h in halves:
            z2_woven = new("z2_woven%d" % h, [P, PACK * HALF], BF16, reuse="a_n1_%d" % (2 + h))
            weave(z2_woven, z2_planes[:, :, cols(h)])
            quantise(z2_codes[:, cols(h)], z2_scales[:, cols(h)], z2_woven)
            sg = new("sg%d" % h, [P, PACK, HALF], F32)
            z_planes = new("z_planes%d" % h, [P, PACK, HALF], BF16)
            for t in tiles:
                nc.scalar.activation(
                    sg[:, t, :], st_win[t][:].indirect(half_of(n2_t, h)), ACT.Sigmoid,
                    bias=gate_bias[:, t : t + 1], scale=sl_t[:, t : t + 1],
                )
                nc.vector.scalar_tensor_tensor(
                    z_planes[:, t, :], a_bank[t][:, cols(h)], gn_score[:, t : t + 1], sg[:, t, :], ALU.mult, ALU.mult
                )
            z_woven = new("z_woven%d" % h, [P, PACK * HALF], BF16)
            weave(z_woven, z_planes[:])
            z_codes = new("z_codes%d" % h, [P, HALF], U32)
            z_scales = new("z_scales%d" % h, [P, HALF], U8)
            quantise(z_codes[:], z_scales[:], z_woven)
            h_bank.append([])
            for t in tiles:
                bank = psum.tile([P, S], F32, name="h_bank%d_%d" % (h, t), tag=("b_bank%d", "a_bank%d")[h] % t)
                h_bank[h].append(bank[:, 0:HALF])
                w_pass(h_bank[h][t], 1, t, z2_codes[:, cols(h)], z2_scales[:, cols(h)], True, False)
                w_pass(h_bank[h][t], 0, t, z_codes[:], z_scales[:], False, True)

        spare_root = new("spare_root", [P, 1], F32)
        nc.scalar.activation(spare_root[:], sg[:, PACK - 1, 0:1], ACT.Abs_reciprocal_sqrt, bias=0.5)

        r_win = [
            new("r_win%d" % t, [P, S], F32, reuse)
            for t, reuse in enumerate(("z_woven1", "z_codes1", "z_scales1", "z2_codes"))
        ]
        root = per_tile("root", S)
        for h in halves:
            for t in tiles:
                size = new("size%d_%d" % (h, t), [P, HALF], F32, reuse="size%d_%d" % (h, t % 2))
                nc.scalar.activation(size[:], h_bank[h][t], ACT.Abs)
                nc.scalar.activation(root[t][:, cols(h)], size[:], ACT.Abs_reciprocal_sqrt, bias=0.5)
                if h == 1 and t in LATE_TILES:
                    nc.scalar.activation(r_win[t][:, cols(h)], root[t][:, cols(h)], ACT.Square)
                else:
                    nc.vector.tensor_tensor(r_win[t][:, cols(h)], root[t][:, cols(h)], root[t][:, cols(h)], ALU.mult)

        out_rows = out_0.rearrange("(p t) j -> p t j", t=PACK)
        out_words = out_1[0].rearrange("p n t -> p (n t)").bitcast(I32)
        y_codes = new("y_codes", [P, S], U32)
        y_scales = new("y_scales", [P, S], U8)
        for h in halves:
            r_n5 = new("r_n5_%d" % h, [P, PACK, HALF], F32)
            y = new("y%d" % h, [P, PACK, HALF], F32)
            for t in tiles:
                gather(h == 1 or t in LATE_TILES, r_n5[:, t, :], r_win[t], half_of(n5_t, h))
                nc.vector.tensor_tensor(y[:, t, :], h_bank[h][t], r_n5[:, t, :], ALU.mult)
            nc.sync.dma_start(out_rows[:, :, cols(h)], y[:])
            y_woven = new("y_woven%d" % h, [P, PACK * HALF], BF16)
            weave(y_woven, y[:])
            quantise(y_codes[:, cols(h)], y_scales[:, cols(h)], y_woven)
            nc.sync.dma_start(out_words[:, cols(h)], y_codes[:, cols(h)].bitcast(I32))
        for j in range(PACK):
            queue = nc.scalar if j % 2 else nc.sync
            queue.dma_start(out_2[0, j:SCALE_ROWS:PACK, :].bitcast(I32), y_scales[j:P:32, :].bitcast(I32))
